import numpy as np, ml_dtypes
CORES = [22,38,54,62,70,110,23,39,55,63,71,111]
N = 12
GR, GC, HH, WW = 4, 3, 8, 16
def setup_inputs(rng):
    return {"x": rng.standard_normal((N, 128, HH * WW), dtype=np.float32).astype(ml_dtypes.bfloat16), "w": rng.standard_normal((N, 128, 9 * 128), dtype=np.float32).astype(ml_dtypes.bfloat16)}
def setup_inputs_big(rng):
    d = setup_inputs(rng)
    for k in ("x", "w"): d[k] = (d[k].astype(np.float32) * 1024.0).astype(d[k].dtype)
    return d
def setup_inputs_small(rng):
    d = setup_inputs(rng)
    for k in ("x", "w"): d[k] = (d[k].astype(np.float32) * (1 / 1024.0)).astype(d[k].dtype)
    return d
def setup_inputs_apart(rng):
    d = setup_inputs(rng)
    f = (10.0 ** rng.permutation(np.linspace(-1.5, 1.5, N))).astype(np.float32).reshape(N, 1, 1)
    for k in ("x", "w"): d[k] = (d[k].astype(np.float32) * f).astype(d[k].dtype)
    return d
def reference(x, w):
    X = x.astype(np.float64).reshape(GR, GC, 128, HH, WW); W = w.astype(np.float64)
    g = np.concatenate([np.concatenate(list(X[i]), axis=2) for i in range(GR)], axis=1)
    y = np.zeros((N, 128, HH * WW))
    for r in range(N):
        i0, j0 = HH * (r // GC), WW * (r % GC)
        for a in range(3):
            for b in range(3):
                sh = np.roll(g, (-2 * (a - 1), -2 * (b - 1)), axis=(1, 2))[:, i0:i0 + HH, j0:j0 + WW]
                y[r] += W[r][:, 128 * (3 * a + b):128 * (3 * a + b) + 128].T @ sh.reshape(128, HH * WW)
    return {"y": y.astype(ml_dtypes.bfloat16 if x.dtype != np.float64 else np.float64)}

from concourse.bass import DstId, RemoteDMATransfer

GR, GC, HH, WW = 4, 3, 8, 16

SCRATCH = {
    "xt": ("sbuf", [128, HH + 4, WW], "bfloat16"),
    "hl": ("sbuf", [128, HH + 4, 2], "bfloat16"),
    "hr": ("sbuf", [128, HH + 4, 2], "bfloat16"),
    "pk": ("sbuf", [128, 2, HH, 2], "bfloat16"),
    "ws": ("sbuf", [128, 9 * 128], "bfloat16"),
    "ys": ("sbuf", [128, HH, WW], "bfloat16"),
    "acc": ("psum", [128, HH, WW], "float32"),
}
SEMAPHORES = ["s_x", "s_w", "s_pk", "s_rows", "s_cols", "s_cor", "s_loc", "s_mm", "s_out", "s_y"]


def _split(engines, parts):
    per = 1
    while per * 2 * parts <= len(engines):
        per *= 2
    masks = []
    for p in range(parts):
        m = 0
        for e in engines[p * per:(p + 1) * per]:
            m |= 1 << e
        masks.append(m)
    return masks, per


def rank_program(g, core, T, topo):
    rank = T.rank_of(core)
    if rank is None:
        return
    S = T.sem
    xt, hl, hr, pk, ws, ys, acc = T.xt, T.hl, T.hr, T.pk, T.ws, T.ys, T.acc

    def nb(dr, dc):
        return T.cores[((rank // GC + dr) % GR) * GC + (rank % GC + dc) % GC]

    allowed = None
    for dr in (-1, 0, 1):
        for dc in (-1, 0, 1):
            if (dr, dc) != (0, 0):
                assert topo.may_write(core, nb(dr, dc))
                m = topo.mask(core, nb(dr, dc))
                allowed = m if allowed is None else allowed & m
    engines = [e for e in range(16) if (allowed >> e) & 1]

    g.sync.dma_start(xt[:, 2:2 + HH, :], T.x[:, :]).then_inc(S.s_x, 16)
    g.sync.dma_start(ws[:, :], T.w[:, :]).then_inc(S.s_w, 16)

    g.vector.wait_ge(S.s_x, 16)
    g.vector.tensor_copy(pk[:, 0], xt[:, 2:2 + HH, 0:2]).then_inc(S.s_pk, 1)
    g.vector.tensor_copy(pk[:, 1], xt[:, 2:2 + HH, WW - 2:WW]).then_inc(S.s_pk, 1)

    sent = [0]

    def send(items, sem):
        masks, per = _split(engines, len(items))
        trs = []
        for (dst_core, dst, src), m in zip(items, masks):
            rid, pid, _ = topo.addr(dst_core)
            trs.append(RemoteDMATransfer(dst_ids=[DstId(rid=rid, pnc=pid)], dma_engine_mask=m, remote_sem=sem,
                                         src=src, dst=dst))
            sent[0] += per
        g.remote_dma_fused(trs, local_sem=S.s_loc)
        return per * len(items)

    g.wait_ge(S.s_x, 16)
    n_rows = send([(nb(-1, 0), xt[:, HH + 2:HH + 4, :], xt[:, 2:4, :]),
                   (nb(+1, 0), xt[:, 0:2, :], xt[:, HH:HH + 2, :])], S.s_rows)
    g.wait_ge(S.s_pk, 2)
    n_cols = send([(nb(0, -1), hr[:, 2:2 + HH, :], pk[:, 0]),
                   (nb(0, +1), hl[:, 2:2 + HH, :], pk[:, 1])], S.s_cols)
    n_cor = send([(nb(-1, -1), hr[:, HH + 2:HH + 4, :], pk[:, 0, 0:2, :]),
                  (nb(-1, +1), hl[:, HH + 2:HH + 4, :], pk[:, 1, 0:2, :]),
                  (nb(+1, -1), hr[:, 0:2, :], pk[:, 0, HH - 2:HH, :]),
                  (nb(+1, +1), hl[:, 0:2, :], pk[:, 1, HH - 2:HH, :])], S.s_cor)

    oc = {0: (2, WW), 1: (0, WW), 2: (0, WW - 2)}
    sc = {0: (0, WW - 2), 1: (0, WW), 2: (2, WW)}
    own = {0: (2, HH), 1: (0, HH), 2: (0, HH - 2)}

    def mid(a, b, i0, i1):
        return (a, b, acc[:, i0:i1, oc[b][0]:oc[b][1]], xt[:, i0 + 2 * a:i1 + 2 * a, sc[b][0]:sc[b][1]])

    early = [mid(1, 1, 0, HH)] + [mid(a, b, own[a][0], own[a][1]) for a in range(3) for b in range(3) if (a, b) != (1, 1)]
    rows = [mid(0, b, 0, 2) for b in range(3)] + [mid(2, b, HH - 2, HH) for b in range(3)]

    def side(a):
        return [(a, 0, acc[:, :, 0:2], hl[:, 2 * a:2 * a + HH, :]), (a, 2, acc[:, :, WW - 2:WW], hr[:, 2 * a:2 * a + HH, :])]

    stages = [([(S.s_x, 16), (S.s_w, 16)], early), ([(S.s_rows, n_rows)], rows), ([(S.s_cols, n_cols)], side(1)),
              ([(S.s_cor, n_cor)], side(0) + side(2))]
    total = sum(len(js) for _, js in stages)
    k = 0
    for waits, js in stages:
        for sem, val in waits:
            g.tensor.wait_ge(sem, val)
        for a, b, out, rhs in js:
            t = 3 * a + b
            g.tensor.matmul(out, ws[:, 128 * t:128 * t + 128], rhs, start=(k == 0), stop=(k == total - 1)).then_inc(S.s_mm, 1)
            k += 1

    g.vector.wait_ge(S.s_mm, total)
    g.vector.tensor_copy(ys[:, :, :], acc[:, :, :]).then_inc(S.s_out, 1)
    g.sync.wait_ge(S.s_out, 1)
    g.sync.dma_start(T.y[:, :], ys[:, :, :]).then_inc(S.s_y, 16)
    g.sync.wait_ge(S.s_y, 16)
    g.wait_ge(S.s_loc, sent[0])
